import numpy as np, ml_dtypes
CORES = [24,25,26,27,48,49,50,51,72,73,74,75,96,97,98,99]
N = 16
import mx_ref
NC, KT = 128, 2
OWNER = [6,3,6,3,6,6,6,3,3,14,6,3,14,6,14,3]
BF = ml_dtypes.bfloat16
def setup_inputs(rng):
    def f(*shape):
        return mx_ref.flush((rng.standard_normal(shape, dtype=np.float32) * np.exp2(rng.integers(-2, 3, shape[:-1] + (1,)))).astype(BF))
    return {"w": f(N, 128, KT * 512), "x": f(N, 128, KT * 4 * NC)}
def setup_inputs_blocks(rng):
    d = setup_inputs(rng)
    for k in ("w", "x"): d[k] = mx_ref.spread(d[k], rng, 4)
    return d
def setup_inputs_wide(rng):
    d = setup_inputs(rng)
    for k in ("w", "x"): d[k] = mx_ref.flush((d[k].astype(np.float32) * np.exp2(rng.integers(-8, 9, (N, 1, 1))).astype(np.float32)).astype(BF))
    return d
def setup_inputs_zeros(rng):
    d = setup_inputs(rng); v = d["x"].reshape(N, 128, -1, 4).copy()
    v[np.broadcast_to((rng.random((N, 1, v.shape[2], 1)) < 0.33), v.shape)] = 0
    d["x"] = v.reshape(d["x"].shape)
    return d
def reference(w, x):
    y = np.zeros((N, 128, NC), np.float32)
    for r in range(N):
        for t in range(KT):
            p = mx_ref.matmul(mx_ref.quantize(w[OWNER[r]][:, 512 * t:512 * t + 512]), mx_ref.quantize(x[r][:, 4 * NC * t:4 * NC * t + 4 * NC]))
            y[r] = p if t == 0 else y[r] + p
    return {"y": y}

@@ -1,0 +1,119 @@
+from concourse.bass import DstId, RemoteDMATransfer
+from concourse.mybir import dt
+
+KT = 2
+COLS = 128
+WORDS = KT * COLS
+
+SCRATCH = {
+    "wb": ("sbuf", [128, KT * 4 * COLS], "bfloat16"),
+    "xb": ("sbuf", [128, KT * 4 * COLS], "bfloat16"),
+    "wq": ("sbuf", [128, WORDS], "float8_e4m3fn_x4"),
+    "ws": ("sbuf", [128, WORDS], "uint8"),
+    "xq": ("sbuf", [128, WORDS], "float8_e4m3fn_x4"),
+    "xs": ("sbuf", [128, WORDS], "uint8"),
+    "acc": ("psum", [128, 512], "float32"),
+    "yb": ("sbuf", [128, COLS], "float32"),
+}
+SEMAPHORES = ["lw0", "lw1", "lx", "qw", "qx", "codes", "plane", "sent", "mm", "cp", "st"]
+
+
+def _count(mask):
+    return bin(mask).count("1")
+
+
+def _tree(holder, users, topo):
+    by_chip = {}
+    for c in users:
+        by_chip.setdefault(topo.chip(c), []).append(c)
+    near = by_chip.pop(topo.chip(holder), [])
+    groups = sorted(by_chip.values(), key=lambda v: -len(v))
+    tree = {holder: ([v[0] for v in groups], near)}
+    for v in groups:
+        if len(v) > 1:
+            tree[v[0]] = ([], v[1:])
+    return tree
+
+
+def _masks(core, far, near, topo):
+    far_mask = near_mask = 0
+    for c in far:
+        far_mask = topo.mask(core, c) if not far_mask else far_mask & topo.mask(core, c)
+    for c in near:
+        near_mask = topo.mask(core, c) if not near_mask else near_mask & topo.mask(core, c)
+    return far_mask, near_mask & ~far_mask
+
+
+def rank_program(g, core, T, topo):
+    rank = T.rank_of(core)
+    if rank is None:
+        return
+    S = T.sem
+    owner = T.tables["OWNER"]
+    o = owner[rank]
+    holder = T.cores[o]
+    users = [T.cores[r] for r in range(len(T.cores)) if owner[r] == o and r != o]
+    tree = _tree(holder, users, topo)
+    holds = core == holder
+
+    if holds:
+        g.sync.dma_start(T.wb[:, 0:512], T.w[:, 0:512]).then_inc(S.lw0, 16)
+        g.scalar.dma_start(T.wb[:, 512:1024], T.w[:, 512:1024]).then_inc(S.lw1, 16)
+    g.sync.dma_start(T.xb[:], T.x[:]).then_inc(S.lx, 16)
+
+    if holds:
+        for t, sem in enumerate((S.lw0, S.lw1)):
+            g.vector.wait_ge(sem, 16)
+            g.vector.quantize_mx(T.wq[:, COLS * t:COLS * (t + 1)], T.ws[:, COLS * t:COLS * (t + 1)],
+                                 T.wb[:, 512 * t:512 * (t + 1)]).then_inc(S.qw, 1)
+    g.vector.wait_ge(S.lx, 16)
+    for t in range(KT):
+        g.vector.quantize_mx(T.xq[:, COLS * t:COLS * (t + 1)], T.xs[:, COLS * t:COLS * (t + 1)],
+                             T.xb[:, 512 * t:512 * (t + 1)]).then_inc(S.qx, 1)
+
+    got = 0
+    for sender, (far, near) in tree.items():
+        fm, nm = _masks(sender, far, near, topo)
+        if core in far:
+            got = _count(fm)
+        if core in near:
+            got = _count(nm)
+
+    if core in tree:
+        far, near = tree[core]
+        fm, nm = _masks(core, far, near, topo)
+        left = 0
+        for part, sem in ((T.wq[:].bitcast(dt.uint8), S.codes), (T.ws[:], S.plane)):
+            if holds:
+                g.wait_ge(S.qw, KT)
+            else:
+                g.wait_ge(sem, got)
+            transfers = []
+            for dsts, m in ((far, fm), (near, nm)):
+                if not dsts:
+                    continue
+                assert all(topo.may_write(core, c) for c in dsts)
+                ids = [DstId(rid=topo.addr(c)[0], pnc=topo.addr(c)[1]) for c in dsts]
+                transfers.append(RemoteDMATransfer(dst_ids=ids, dma_engine_mask=m, remote_sem=sem,
+                                                   srcs=[part], dsts=[part for _ in dsts]))
+                left += _count(m)
+            g.remote_dma_fused(transfers, local_sem=S.sent)
+        g.wait_ge(S.sent, left)
+
+    g.tensor.wait_ge(S.qx, KT)
+    if holds:
+        g.tensor.wait_ge(S.qw, KT)
+    else:
+        g.tensor.wait_ge(S.codes, got)
+        g.tensor.wait_ge(S.plane, got)
+    for t in range(KT):
+        sl = slice(COLS * t, COLS * (t + 1))
+        mmv = g.tensor.matmul_mx(T.acc[:, 0:COLS], T.wq[:, sl], T.ws[:, sl], T.xq[:, sl], T.xs[:, sl],
+                                 t == 0, t == KT - 1)
+    mmv.then_inc(S.mm, 1)
+
+    g.vector.wait_ge(S.mm, 1)
+    g.vector.tensor_copy(T.yb[:], T.acc[:, 0:COLS]).then_inc(S.cp, 1)
+    g.sync.wait_ge(S.cp, 1)
+    g.sync.dma_start(T.y[:], T.yb[:]).then_inc(S.st, 16)
+    g.sync.wait_ge(S.st, 16)

@@ -4,6 +4,7 @@ from concourse.mybir import dt
 KT = 2
 COLS = 128
 WORDS = KT * COLS
+DIRECT = 2
 
 SCRATCH = {
     "wb": ("sbuf", [128, KT * 4 * COLS], "bfloat16"),
@@ -15,84 +16,102 @@ SCRATCH = {
     "acc": ("psum", [128, 512], "float32"),
     "yb": ("sbuf", [128, COLS], "float32"),
 }
-SEMAPHORES = ["lw0", "lw1", "lx", "qw", "qx", "codes", "plane", "sent", "mm", "cp", "st"]
+SEMAPHORES = ["lw0", "lw1", "lx", "qw0", "qw1", "qx", "codes0", "codes1", "plane", "sent", "mm", "cp", "st"]
 
 
 def _count(mask):
     return bin(mask).count("1")
 
 
-def _tree(holder, users, topo):
-    by_chip = {}
-    for c in users:
-        by_chip.setdefault(topo.chip(c), []).append(c)
-    near = by_chip.pop(topo.chip(holder), [])
-    groups = sorted(by_chip.values(), key=lambda v: -len(v))
-    tree = {holder: ([v[0] for v in groups], near)}
-    for v in groups:
-        if len(v) > 1:
-            tree[v[0]] = ([], v[1:])
-    return tree
+def _common(core, dsts, topo):
+    m = 0
+    for c in dsts:
+        m = topo.mask(core, c) if not m else m & topo.mask(core, c)
+    return m
 
 
-def _masks(core, far, near, topo):
-    far_mask = near_mask = 0
-    for c in far:
-        far_mask = topo.mask(core, c) if not far_mask else far_mask & topo.mask(core, c)
-    for c in near:
-        near_mask = topo.mask(core, c) if not near_mask else near_mask & topo.mask(core, c)
-    return far_mask, near_mask & ~far_mask
+def _plan(cores, owner, topo):
+    jobs = []
+    for o in sorted(set(owner)):
+        h = cores[o]
+        by_chip = {}
+        for r, c in enumerate(cores):
+            if owner[r] == o and c != h:
+                by_chip.setdefault(topo.chip(c), []).append(c)
+        near = by_chip.pop(topo.chip(h), [])
+        jobs.append((h, near, sorted(by_chip.values(), key=lambda v: -len(v))))
+    jobs.sort(key=lambda j: -len(j[2]))
+    entered, taken, sends = {}, set(cores), {}
+    for h, near, groups in jobs:
+        far, porters = [], []
+        home = [c for c in range(topo.CHIPS * topo.CORES_PER_CHIP) if topo.chip(c) == topo.chip(h)]
+        for v in groups:
+            lead = v[0]
+
+            def free(c):
+                return topo.may_write(c, lead) and entered.get((topo.chip(lead), topo.die(c)), 0) < DIRECT
+            if len(far) < DIRECT and free(h):
+                far.append(lead)
+                via = h
+            else:
+                cand = [c for c in near if c not in porters and free(c)]
+                cand += [c for c in home if c not in taken and topo.die(c) != topo.die(h) and free(c)]
+                via = cand[0]
+                porters.append(via)
+                taken.add(via)
+                sends[via] = [([lead], topo.mask(via, lead))]
+            port = (topo.chip(lead), topo.die(via))
+            entered[port] = entered.get(port, 0) + 1
+            if len(v) > 1:
+                sends[lead] = [(v[1:], _common(lead, v[1:], topo))]
+        stay = porters + [c for c in near if c not in porters]
+        far_mask = _common(h, far, topo)
+        sends[h] = [(far, far_mask), (stay, _common(h, stay, topo) & ~far_mask)]
+    return sends
 
 
 def rank_program(g, core, T, topo):
-    rank = T.rank_of(core)
-    if rank is None:
-        return
     S = T.sem
+    rank = T.rank_of(core)
     owner = T.tables["OWNER"]
-    o = owner[rank]
-    holder = T.cores[o]
-    users = [T.cores[r] for r in range(len(T.cores)) if owner[r] == o and r != o]
-    tree = _tree(holder, users, topo)
-    holds = core == holder
-
-    if holds:
-        g.sync.dma_start(T.wb[:, 0:512], T.w[:, 0:512]).then_inc(S.lw0, 16)
-        g.scalar.dma_start(T.wb[:, 512:1024], T.w[:, 512:1024]).then_inc(S.lw1, 16)
-    g.sync.dma_start(T.xb[:], T.x[:]).then_inc(S.lx, 16)
-
-    if holds:
-        for t, sem in enumerate((S.lw0, S.lw1)):
-            g.vector.wait_ge(sem, 16)
-            g.vector.quantize_mx(T.wq[:, COLS * t:COLS * (t + 1)], T.ws[:, COLS * t:COLS * (t + 1)],
-                                 T.wb[:, 512 * t:512 * (t + 1)]).then_inc(S.qw, 1)
-    g.vector.wait_ge(S.lx, 16)
-    for t in range(KT):
-        g.vector.quantize_mx(T.xq[:, COLS * t:COLS * (t + 1)], T.xs[:, COLS * t:COLS * (t + 1)],
-                             T.xb[:, 512 * t:512 * (t + 1)]).then_inc(S.qx, 1)
+    sends = _plan(T.cores, owner, topo)
+    holds = rank is not None and rank in owner
 
     got = 0
-    for sender, (far, near) in tree.items():
-        fm, nm = _masks(sender, far, near, topo)
-        if core in far:
-            got = _count(fm)
-        if core in near:
-            got = _count(nm)
+    for transfers in sends.values():
+        for dsts, m in transfers:
+            if core in dsts:
+                got = _count(m)
 
-    if core in tree:
-        far, near = tree[core]
-        fm, nm = _masks(core, far, near, topo)
+    if rank is not None:
+        if holds:
+            g.sync.dma_start(T.wb[:, 0:512], T.w[:, 0:512]).then_inc(S.lw0, 16)
+            g.scalar.dma_start(T.wb[:, 512:1024], T.w[:, 512:1024]).then_inc(S.lw1, 16)
+        g.sync.dma_start(T.xb[:], T.x[:]).then_inc(S.lx, 16)
+
+        if holds:
+            for t, (sem, done) in enumerate(((S.lw0, S.qw0), (S.lw1, S.qw1))):
+                g.vector.wait_ge(sem, 16)
+                g.vector.quantize_mx(T.wq[:, COLS * t:COLS * (t + 1)], T.ws[:, COLS * t:COLS * (t + 1)],
+                                     T.wb[:, 512 * t:512 * (t + 1)]).then_inc(done, 1)
+        g.vector.wait_ge(S.lx, 16)
+        for t in range(KT):
+            g.vector.quantize_mx(T.xq[:, COLS * t:COLS * (t + 1)], T.xs[:, COLS * t:COLS * (t + 1)],
+                                 T.xb[:, 512 * t:512 * (t + 1)]).then_inc(S.qx, 1)
+
+    if core in sends:
         left = 0
-        for part, sem in ((T.wq[:].bitcast(dt.uint8), S.codes), (T.ws[:], S.plane)):
+        for part, sem, packed in ((T.wq[:, 0:COLS].bitcast(dt.uint8), S.codes0, S.qw0),
+                                  (T.ws[:], S.plane, S.qw1),
+                                  (T.wq[:, COLS:WORDS].bitcast(dt.uint8), S.codes1, S.qw1)):
             if holds:
-                g.wait_ge(S.qw, KT)
+                g.wait_ge(packed, 1)
             else:
                 g.wait_ge(sem, got)
             transfers = []
-            for dsts, m in ((far, fm), (near, nm)):
+            for dsts, m in sends[core]:
                 if not dsts:
                     continue
-                assert all(topo.may_write(core, c) for c in dsts)
                 ids = [DstId(rid=topo.addr(c)[0], pnc=topo.addr(c)[1]) for c in dsts]
                 transfers.append(RemoteDMATransfer(dst_ids=ids, dma_engine_mask=m, remote_sem=sem,
                                                    srcs=[part], dsts=[part for _ in dsts]))
@@ -100,13 +119,17 @@ def rank_program(g, core, T, topo):
             g.remote_dma_fused(transfers, local_sem=S.sent)
         g.wait_ge(S.sent, left)
 
+    if rank is None:
+        return
+
     g.tensor.wait_ge(S.qx, KT)
-    if holds:
-        g.tensor.wait_ge(S.qw, KT)
-    else:
-        g.tensor.wait_ge(S.codes, got)
-        g.tensor.wait_ge(S.plane, got)
     for t in range(KT):
+        if holds:
+            g.tensor.wait_ge((S.qw0, S.qw1)[t], 1)
+        else:
+            if t == 0:
+                g.tensor.wait_ge(S.plane, got)
+            g.tensor.wait_ge((S.codes0, S.codes1)[t], got)
         sl = slice(COLS * t, COLS * (t + 1))
         mmv = g.tensor.matmul_mx(T.acc[:, 0:COLS], T.wq[:, sl], T.ws[:, sl], T.xq[:, sl], T.xs[:, sl],
                                  t == 0, t == KT - 1)

from concourse.bass import DstId, RemoteDMATransfer
from concourse.mybir import dt

KT = 2
COLS = 128
WORDS = KT * COLS
DIRECT = 2

SCRATCH = {
    "wb": ("sbuf", [128, KT * 4 * COLS], "bfloat16"),
    "xb": ("sbuf", [128, KT * 4 * COLS], "bfloat16"),
    "wq": ("sbuf", [128, WORDS], "float8_e4m3fn_x4"),
    "ws": ("sbuf", [128, WORDS], "uint8"),
    "xq": ("sbuf", [128, WORDS], "float8_e4m3fn_x4"),
    "xs": ("sbuf", [128, WORDS], "uint8"),
    "acc": ("psum", [128, 512], "float32"),
    "yb": ("sbuf", [128, COLS], "float32"),
}
SEMAPHORES = ["lw0", "lw1", "lx", "qw0", "qw1", "qx", "codes0", "codes1", "plane", "sent", "mm", "cp", "st"]


def _count(mask):
    return bin(mask).count("1")


def _common(core, dsts, topo):
    m = 0
    for c in dsts:
        m = topo.mask(core, c) if not m else m & topo.mask(core, c)
    return m


def _plan(cores, owner, topo):
    jobs = []
    for o in sorted(set(owner)):
        h = cores[o]
        by_chip = {}
        for r, c in enumerate(cores):
            if owner[r] == o and c != h:
                by_chip.setdefault(topo.chip(c), []).append(c)
        near = by_chip.pop(topo.chip(h), [])
        jobs.append((h, near, sorted(by_chip.values(), key=lambda v: -len(v))))
    jobs.sort(key=lambda j: -len(j[2]))
    entered, taken, sends = {}, set(cores), {}
    for h, near, groups in jobs:
        far, porters = [], []
        home = [c for c in range(topo.CHIPS * topo.CORES_PER_CHIP) if topo.chip(c) == topo.chip(h)]
        for v in groups:
            lead = v[0]

            def free(c):
                return topo.may_write(c, lead) and entered.get((topo.chip(lead), topo.die(c)), 0) < DIRECT
            if len(far) < DIRECT and free(h):
                far.append(lead)
                via = h
            else:
                cand = [c for c in near if c not in porters and free(c)]
                cand += [c for c in home if c not in taken and topo.die(c) != topo.die(h) and free(c)]
                via = cand[0]
                porters.append(via)
                taken.add(via)
                sends[via] = [([lead], topo.mask(via, lead))]
            port = (topo.chip(lead), topo.die(via))
            entered[port] = entered.get(port, 0) + 1
            if len(v) > 1:
                sends[lead] = [(v[1:], _common(lead, v[1:], topo))]
        stay = porters + [c for c in near if c not in porters]
        far_mask = _common(h, far, topo)
        sends[h] = [(far, far_mask), (stay, _common(h, stay, topo) & ~far_mask)]
    return sends


def rank_program(g, core, T, topo):
    S = T.sem
    rank = T.rank_of(core)
    owner = T.tables["OWNER"]
    sends = _plan(T.cores, owner, topo)
    holds = rank is not None and rank in owner

    got = 0
    for transfers in sends.values():
        for dsts, m in transfers:
            if core in dsts:
                got = _count(m)

    if rank is not None:
        if holds:
            g.sync.dma_start(T.wb[:, 0:512], T.w[:, 0:512]).then_inc(S.lw0, 16)
            g.scalar.dma_start(T.wb[:, 512:1024], T.w[:, 512:1024]).then_inc(S.lw1, 16)
        g.sync.dma_start(T.xb[:], T.x[:]).then_inc(S.lx, 16)

        if holds:
            for t, (sem, done) in enumerate(((S.lw0, S.qw0), (S.lw1, S.qw1))):
                g.vector.wait_ge(sem, 16)
                g.vector.quantize_mx(T.wq[:, COLS * t:COLS * (t + 1)], T.ws[:, COLS * t:COLS * (t + 1)],
                                     T.wb[:, 512 * t:512 * (t + 1)]).then_inc(done, 1)
        g.vector.wait_ge(S.lx, 16)
        for t in range(KT):
            g.vector.quantize_mx(T.xq[:, COLS * t:COLS * (t + 1)], T.xs[:, COLS * t:COLS * (t + 1)],
                                 T.xb[:, 512 * t:512 * (t + 1)]).then_inc(S.qx, 1)

    if core in sends:
        left = 0
        for part, sem, packed in ((T.wq[:, 0:COLS].bitcast(dt.uint8), S.codes0, S.qw0),
                                  (T.ws[:], S.plane, S.qw1),
                                  (T.wq[:, COLS:WORDS].bitcast(dt.uint8), S.codes1, S.qw1)):
            if holds:
                g.wait_ge(packed, 1)
            else:
                g.wait_ge(sem, got)
            transfers = []
            for dsts, m in sends[core]:
                if not dsts:
                    continue
                ids = [DstId(rid=topo.addr(c)[0], pnc=topo.addr(c)[1]) for c in dsts]
                transfers.append(RemoteDMATransfer(dst_ids=ids, dma_engine_mask=m, remote_sem=sem,
                                                   srcs=[part], dsts=[part for _ in dsts]))
                left += _count(m)
            g.remote_dma_fused(transfers, local_sem=S.sent)
        g.wait_ge(S.sent, left)

    if rank is None:
        return

    g.tensor.wait_ge(S.qx, KT)
    for t in range(KT):
        if holds:
            g.tensor.wait_ge((S.qw0, S.qw1)[t], 1)
        else:
            if t == 0:
                g.tensor.wait_ge(S.plane, got)
            g.tensor.wait_ge((S.codes0, S.codes1)[t], got)
        sl = slice(COLS * t, COLS * (t + 1))
        mmv = g.tensor.matmul_mx(T.acc[:, 0:COLS], T.wq[:, sl], T.ws[:, sl], T.xq[:, sl], T.xs[:, sl],
                                 t == 0, t == KT - 1)
    mmv.then_inc(S.mm, 1)

    g.vector.wait_ge(S.mm, 1)
    g.vector.tensor_copy(T.yb[:], T.acc[:, 0:COLS]).then_inc(S.cp, 1)
    g.sync.wait_ge(S.cp, 1)
    g.sync.dma_start(T.y[:], T.yb[:]).then_inc(S.st, 16)
    g.sync.wait_ge(S.st, 16)
